import numpy as np, ml_dtypes
CORES = [19,27,51,107,147,155,179,235,275,283,307,363,403,411,435,491]
N = 16
KT, C = 8, 64
def setup_inputs(rng):
    return {"x": rng.standard_normal((N, 128, KT * C), dtype=np.float32).astype(ml_dtypes.bfloat16)}
def setup_inputs_big(rng):
    d = setup_inputs(rng)
    for k in ("x",): d[k] = (d[k].astype(np.float32) * 1024.0).astype(d[k].dtype)
    return d
def setup_inputs_small(rng):
    d = setup_inputs(rng)
    for k in ("x",): d[k] = (d[k].astype(np.float32) * (1 / 1024.0)).astype(d[k].dtype)
    return d
def setup_inputs_apart(rng):
    d = setup_inputs(rng)
    f = (10.0 ** rng.permutation(np.linspace(-1.5, 1.5, N))).astype(np.float32).reshape(N, 1, 1)
    for k in ("x",): d[k] = (d[k].astype(np.float32) * f).astype(d[k].dtype)
    return d
def reference(x):
    X = x.astype(np.float64)
    y = np.full((N, C, N * C), np.nan)
    for r in range(N):
        for i in range(N):
            s = i
            if s != r: y[r][:, C * i:C * i + C] = sum(X[r][:, C * t:C * t + C].T @ X[s][:, C * t:C * t + C] for t in range(KT))
    return {"y": y.astype(ml_dtypes.bfloat16 if x.dtype != np.float64 else np.float64)}

@@ -1,0 +1,215 @@
+from concourse.bass import DstId, RemoteDMATransfer
+
+KT, CB = 8, 64
+SCRATCH = {
+    "X": ("sbuf", [128, 6, KT, CB], "bfloat16"),
+    "pBR": ("psum", [128, 512], "float32"), "pBI": ("psum", [128, 512], "float32"),
+    "pCR": ("psum", [128, 512], "float32"), "pCI": ("psum", [128, 512], "float32"),
+    "pOR": ("psum", [128, 512], "float32"), "pOI": ("psum", [128, 512], "float32"),
+    "p1": ("psum", [128, 512], "float32"),
+    "ZBR": ("sbuf", [128, 2 * CB], "bfloat16"),
+    "ZBI": ("sbuf", [128, 2 * CB], "bfloat16"),
+    "ZC": ("sbuf", [128, 2 * CB], "bfloat16"),
+    "ZO": ("sbuf", [128, 5 * CB], "bfloat16"),
+    "LC": ("sbuf", [128, 2 * CB], "bfloat16"),
+    "LR": ("sbuf", [128, 2, 2 * CB], "bfloat16"),
+    "LI": ("sbuf", [128, 2, 2 * CB], "bfloat16"),
+}
+SEMAPHORES = ["ld", "a1", "a2", "a3", "a4", "a5", "snt", "ms", "mBR", "mBI", "mCR", "mCI", "mOR", "mOI", "m1",
+              "cBR", "cBI", "cCR", "cCI", "cOR", "cOI", "c1", "rC", "rR0", "rR1", "rI0", "rI1", "st"]
+_CACHE = {}
+
+
+def _bits(m):
+    return [e for e in range(32) if (m >> e) & 1]
+
+
+def _plan(cores, topo):
+    if "p" in _CACHE:
+        return _CACHE["p"]
+    n = len(cores)
+    rk = range(n)
+    host = [topo.host(c) for c in cores]
+    rack = [topo.rack(h) for h in host]
+    same_host = lambda a, b: host[a] == host[b]
+    C = [[s for s in rk if rack[s] != rack[r] and topo.may_write(cores[r], cores[s]) and topo.chip(cores[s]) == topo.chip(cores[r])][0]
+         for r in rk]
+    mine = [[s for s in rk if same_host(r, s)] for r in rk]
+    half = [int(not any(topo.mates(cores[r], cores[s]) for s in mine[r])) for r in rk]
+    pos = [mine[r].index(r) for r in rk]
+    low = [host[r] in (host[0], host[C[0]]) for r in rk]
+    nb = [[s for s in rk if rack[s] == rack[r] and not same_host(r, s)] for r in rk]
+    W2 = [[s for s in nb[r] if (half[s] != half[r]) == low[r]] for r in rk]
+
+    def route(a, b):
+        ca, cb = cores[a], cores[b]
+        if rack[a] != rack[b]:
+            return [("cable", a)]
+        if topo.mates(ca, cb):
+            return [("mate", a)]
+        if topo.same_plane(ca, cb):
+            return [("out", a), ("in", b)]
+        m = [s for s in mine[a] if topo.mates(ca, cores[s])]
+        return [("mate", a), ("out", m[0] if m else ("mate of", a)), ("in", b)]
+
+    k = len(mine[0])
+    pairs = [(i, j) for i in range(k) for j in range(i + 1, k)]
+    best = None
+    for code in range(1 << len(pairs)):
+        arcs = [(p if (code >> q) & 1 else (p[1], p[0])) for q, p in enumerate(pairs)]
+        sends = [(r, C[r]) for r in rk] + [(r, s) for r in rk for s in W2[r]]
+        sends += [(mine[r][i], mine[r][j]) for r in rk if pos[r] == 0 for i, j in arcs]
+        load, got = {}, [0] * n
+        for a, b in sends:
+            got[b] += 1
+            for l in route(a, b):
+                load[l] = load.get(l, 0) + 1
+        top = lambda kind: max(v for l, v in load.items() if l[0] == kind)
+        score = (max(got), top("in"), top("out"), top("mate"), sum(v * v for v in load.values()), code)
+        if best is None or score < best[0]:
+            best = (score, arcs)
+    arcs = best[1]
+    W3 = [sorted(mine[r][j] for i, j in arcs if i == pos[r]) for r in rk]
+    R = [[s for s in rk if r in W2[s]] for r in rk]
+    I = [[s for s in rk if r in W3[s]] for r in rk]
+    XS = []
+    for r in rk:
+        w3 = sorted(W3[r], key=lambda s: (len(I[s]), s))
+        XS.append([[(C[r], 4), (w3[0], 4)], [(d, 4) for d in W2[r]]] + [[(d, 8)] for d in w3[1:]])
+    due = {}
+    for r in rk:
+        t = 0
+        for call in XS[r]:
+            t += 128 // call[0][1]
+            for d, ne in call:
+                due[(r, d)] = t
+    p = {"C": C, "R": R, "I": I, "W2": W2, "W3": W3, "XS": XS, "due": due}
+    _CACHE["p"] = p
+    return p
+
+
+def rank_program(g, core, T, topo):
+    r = T.rank_of(core)
+    if r is None:
+        return
+    cores = list(T.cores)
+    P = _plan(cores, topo)
+    C, R, I, W2, W3, XS, due = P["C"], P["R"], P["I"], P["W2"], P["W3"], P["XS"], P["due"]
+    S = T.sem
+    X = T.X
+    ni = len(I[r])
+    sent = [0]
+
+    def slot_at(v, s):
+        return 1 if s == C[v] else (2 + R[v].index(s) if s in R[v] else 4 + I[v].index(s))
+
+    def ready(v, fam):
+        return max([due[(C[v], v)]] + [due[(s, v)] for s in (R[v] if fam == "R" else I[v])])
+
+    def fused(items):
+        trs = []
+        for j, (d, ne, src, dst, sem) in enumerate(items):
+            rid, pid = topo.addr(cores[d], core)
+            eng = _bits(topo.mask(core, cores[d]))[j::len(items)][:ne]
+            trs.append(RemoteDMATransfer(dst_ids=[DstId(rid=rid, pnc=pid)], dma_engine_mask=sum(1 << e for e in eng),
+                                         remote_sem=sem, src=src, dst=dst))
+            sent[0] += ne
+        g.remote_dma_fused(trs, local_sem=S.snt)
+
+    def x_engines(s):
+        return [ne for call in XS[s] for d, ne in call if d == r][0]
+
+    g.sync.dma_start(X[:, 0], T.x[:]).then_inc(S.ld, 16)
+    if ni == 1:
+        g.vector.memset(T.ZBI[CB:2 * CB, :], 0.0).then_inc(S.ms, 1)
+        g.vector.memset(T.ZC[0:CB, CB:2 * CB], 0.0).then_inc(S.ms, 1)
+    g.wait_ge(S.ld, 16)
+    for call in XS[r]:
+        fused([(d, ne, X[:, 0], X[:, slot_at(d, r)], S["a%d" % slot_at(d, r)]) for d, ne in call])
+
+    fams = sorted(["I", "R"], key=lambda f: ready(r, f))
+    F = {"R": dict(guests=R[r], s0=2, lo=CB, oc=0), "I": dict(guests=I[r], s0=4, lo=0, oc=2 * CB)}
+
+    te, ve = g.tensor, g.vector
+
+    def group(out, lo, l, r0, r1, sem=None):
+        for t in range(KT):
+            rhs = X[:, r0:r1, t, :] if r1 - r0 > 1 else X[:, r0, t, :]
+            mm = te.matmul(out[lo:lo + CB, 0:CB * (r1 - r0)], X[:, l, t, :], rhs, t == 0, t == KT - 1)
+        if sem is not None:
+            mm.then_inc(sem, 1)
+
+    def rounded(msem, csem, out, in_):
+        ve.wait_ge(msem, 1)
+        ve.tensor_copy(out, in_).then_inc(csem, 1)
+
+    te.wait_ge(S.ld, 16)
+    te.wait_ge(S.a1, x_engines(C[r]))
+    for q, fn in enumerate(fams):
+        f = F[fn]
+        k, s0, lo = len(f["guests"]), f["s0"], f["lo"]
+        for j, s in enumerate(f["guests"]):
+            te.wait_ge(S["a%d" % (s0 + j)], x_engines(s))
+        for j in range(k):
+            group(T["pB" + fn], CB * j, s0 + j, 0, 2, S["mB" + fn] if j == k - 1 else None)
+        rounded(S["mB" + fn], S["cB" + fn], T["ZB" + fn][0:CB * k, :], T["pB" + fn][0:CB * k, 0:2 * CB])
+        group(T["pC" + fn], lo, 1, s0, s0 + k, S["mC" + fn])
+        rounded(S["mC" + fn], S["cC" + fn], T.ZC[lo:lo + CB, 0:CB * k], T["pC" + fn][lo:lo + CB, 0:CB * k])
+        group(T["pO" + fn], 0, 0, s0, s0 + k, S["mO" + fn])
+        rounded(S["mO" + fn], S["cO" + fn], T.ZO[0:CB, f["oc"]:f["oc"] + CB * k], T["pO" + fn][0:CB, 0:CB * k])
+        if q == 0:
+            group(T.p1, 0, 0, 1, 2, S.m1)
+            rounded(S.m1, S.c1, T.ZO[0:CB, 4 * CB:5 * CB], T.p1[0:CB, 0:CB])
+
+    for fn in fams:
+        g.wait_ge(S["cB" + fn], 1)
+        if fn == "R":
+            fused([(d, 4, T.ZBR[:, :], T.LR[:, W2[d].index(r)], S["rR%d" % W2[d].index(r)]) for d in R[r]])
+        else:
+            if ni == 1:
+                g.wait_ge(S.ms, 2)
+            fused([(d, 8 // ni, T.ZBI[:, :], T.LI[:, W3[d].index(r)], S["rI%d" % W3[d].index(r)]) for d in I[r]])
+    g.wait_ge(S.cCR, 1)
+    g.wait_ge(S.cCI, 1)
+    fused([(C[r], 8, T.ZC[:, :], T.LC[:, :], S.rC)])
+
+    nst = [0]
+    qs = [g.sync, g.scalar]
+
+    def store(sem, val, pieces):
+        for s, src, k in pieces:
+            q = qs[nst[0] % 2]
+            q.wait_ge(sem, val)
+            q.dma_start(T.y[:, CB * s:CB * (s + k)], src).then_inc(S.st, 16)
+            nst[0] += 1
+
+    def runs(blocks, tile, lo, off):
+        out, j = [], 0
+        while j < len(blocks):
+            k = 1
+            while j + k < len(blocks) and blocks[j + k] == blocks[j] + k:
+                k += 1
+            out.append((blocks[j], tile[lo:lo + CB, off + CB * j:off + CB * (j + k)], k))
+            j += k
+        return out
+
+    for q, fn in enumerate(fams):
+        store(S["cO" + fn], 1, runs(F[fn]["guests"], T.ZO, 0, F[fn]["oc"]))
+        if q == 0:
+            store(S.c1, 1, runs([C[r]], T.ZO, 0, 4 * CB))
+    back = []
+    for j, v in enumerate(W2[r]):
+        lo = CB * R[v].index(r)
+        back.append(((ready(v, "R"), 0, v), S["rR%d" % j], 4,
+                     [(v, T.LR[lo:lo + CB, j, 0:CB], 1), (C[v], T.LR[lo:lo + CB, j, CB:2 * CB], 1)]))
+    for j, v in enumerate(W3[r]):
+        lo = CB * I[v].index(r)
+        back.append(((ready(v, "I"), 0, v), S["rI%d" % j], 8 // len(I[v]),
+                     [(v, T.LI[lo:lo + CB, j, 0:CB], 1), (C[v], T.LI[lo:lo + CB, j, CB:2 * CB], 1)]))
+    v = C[r]
+    back.append(((max(ready(v, "R"), ready(v, "I")), 1, v), S.rC, 8, runs(R[v], T.LC, CB, 0) + runs(I[v], T.LC, 0, 0)))
+    for key, sem, val, pieces in sorted(back, key=lambda b: b[0]):
+        store(sem, val, pieces)
+
+    g.wait_ge(S.snt, sent[0])
+    g.wait_ge(S.st, 16 * nst[0])

@@ -1,22 +1,21 @@
 from concourse.bass import DstId, RemoteDMATransfer
 
-KT, CB = 8, 64
+KT, CB, NG = 8, 64, 4
 SCRATCH = {
     "X": ("sbuf", [128, 6, KT, CB], "bfloat16"),
-    "pBR": ("psum", [128, 512], "float32"), "pBI": ("psum", [128, 512], "float32"),
-    "pCR": ("psum", [128, 512], "float32"), "pCI": ("psum", [128, 512], "float32"),
-    "pOR": ("psum", [128, 512], "float32"), "pOI": ("psum", [128, 512], "float32"),
-    "p1": ("psum", [128, 512], "float32"),
-    "ZBR": ("sbuf", [128, 2 * CB], "bfloat16"),
-    "ZBI": ("sbuf", [128, 2 * CB], "bfloat16"),
+    "XV": ("sbuf", [128, KT, 3 * CB], "bfloat16"),
+    "ZB": ("sbuf", [128, NG, CB], "bfloat16"),
+    "ZO": ("sbuf", [128, NG * CB], "bfloat16"),
     "ZC": ("sbuf", [128, 2 * CB], "bfloat16"),
-    "ZO": ("sbuf", [128, 5 * CB], "bfloat16"),
+    "Z1": ("sbuf", [128, CB], "bfloat16"),
+    "LB": ("sbuf", [128, NG, CB], "bfloat16"),
     "LC": ("sbuf", [128, 2 * CB], "bfloat16"),
-    "LR": ("sbuf", [128, 2, 2 * CB], "bfloat16"),
-    "LI": ("sbuf", [128, 2, 2 * CB], "bfloat16"),
 }
-SEMAPHORES = ["ld", "a1", "a2", "a3", "a4", "a5", "snt", "ms", "mBR", "mBI", "mCR", "mCI", "mOR", "mOI", "m1",
-              "cBR", "cBI", "cCR", "cCI", "cOR", "cOI", "c1", "rC", "rR0", "rR1", "rI0", "rI1", "st"]
+SEMAPHORES = ["ld", "a1", "a2", "a3", "a4", "a5", "snt", "iV", "ms", "m1", "c1", "rC0", "rC1", "st"]
+for _q in range(NG):
+    SCRATCH["pB%d" % _q] = ("psum", [128, 512], "float32")
+    SCRATCH["pV%d" % _q] = ("psum", [128, 512], "float32")
+    SEMAPHORES += ["mB%d" % _q, "mV%d" % _q, "cB%d" % _q, "cV%d" % _q, "cC%d" % _q, "rB%d" % _q]
 _CACHE = {}
 
 
@@ -72,18 +71,27 @@ def _plan(cores, topo):
     W3 = [sorted(mine[r][j] for i, j in arcs if i == pos[r]) for r in rk]
     R = [[s for s in rk if r in W2[s]] for r in rk]
     I = [[s for s in rk if r in W3[s]] for r in rk]
-    XS = []
-    for r in rk:
-        w3 = sorted(W3[r], key=lambda s: (len(I[s]), s))
-        XS.append([[(C[r], 4), (w3[0], 4)], [(d, 4) for d in W2[r]]] + [[(d, 8)] for d in w3[1:]])
-    due = {}
-    for r in rk:
-        t = 0
-        for call in XS[r]:
-            t += 128 // call[0][1]
-            for d, ne in call:
-                due[(r, d)] = t
-    p = {"C": C, "R": R, "I": I, "W2": W2, "W3": W3, "XS": XS, "due": due}
+    HS = [W2[r] + W3[r] for r in rk]
+    GS = [R[r] + I[r] for r in rk]
+    edges = [(s, d) for s in rk for d in HS[s]]
+    turn = {}
+
+    def colour(i):
+        if i == len(edges):
+            return True
+        s, d = edges[i]
+        for c in range(min(len(HS[s]), len(GS[d]))):
+            if all(turn[e] != c for e in edges[:i] if e[0] == s or e[1] == d):
+                turn[(s, d)] = c
+                if colour(i + 1):
+                    return True
+                del turn[(s, d)]
+        return False
+
+    assert colour(0)
+    OUT = [sorted(HS[r], key=lambda d: turn[(r, d)]) for r in rk]
+    ORD = [sorted(GS[r], key=lambda s: turn[(s, r)]) for r in rk]
+    p = {"C": C, "R": R, "I": I, "HS": HS, "OUT": OUT, "ORD": ORD}
     _CACHE["p"] = p
     return p
 
@@ -94,122 +102,117 @@ def rank_program(g, core, T, topo):
         return
     cores = list(T.cores)
     P = _plan(cores, topo)
-    C, R, I, W2, W3, XS, due = P["C"], P["R"], P["I"], P["W2"], P["W3"], P["XS"], P["due"]
+    C, R, I, HS, OUT, ORD = P["C"], P["R"], P["I"], P["HS"], P["OUT"], P["ORD"]
     S = T.sem
-    X = T.X
-    ni = len(I[r])
+    X, XV = T.X, T.XV
+    guests = ORD[r]
+    n = len(guests)
     sent = [0]
 
     def slot_at(v, s):
         return 1 if s == C[v] else (2 + R[v].index(s) if s in R[v] else 4 + I[v].index(s))
 
-    def ready(v, fam):
-        return max([due[(C[v], v)]] + [due[(s, v)] for s in (R[v] if fam == "R" else I[v])])
+    def engines(a, b, j=0, m=1):
+        return _bits(topo.mask(cores[a], cores[b]))[j::m]
+
+    def x_engines(s, d):
+        if d == C[s]:
+            return engines(s, d, 0, 2)
+        return engines(s, d, 1, 2) if d == OUT[s][0] else engines(s, d)
 
     def fused(items):
         trs = []
-        for j, (d, ne, src, dst, sem) in enumerate(items):
+        for d, eng, src, dst, sem in items:
             rid, pid = topo.addr(cores[d], core)
-            eng = _bits(topo.mask(core, cores[d]))[j::len(items)][:ne]
             trs.append(RemoteDMATransfer(dst_ids=[DstId(rid=rid, pnc=pid)], dma_engine_mask=sum(1 << e for e in eng),
                                          remote_sem=sem, src=src, dst=dst))
-            sent[0] += ne
+            sent[0] += len(eng)
         g.remote_dma_fused(trs, local_sem=S.snt)
 
-    def x_engines(s):
-        return [ne for call in XS[s] for d, ne in call if d == r][0]
+    def x_to(d):
+        return (d, x_engines(r, d), X[:, 0], X[:, slot_at(d, r)], S["a%d" % slot_at(d, r)])
 
     g.sync.dma_start(X[:, 0], T.x[:]).then_inc(S.ld, 16)
-    if ni == 1:
-        g.vector.memset(T.ZBI[CB:2 * CB, :], 0.0).then_inc(S.ms, 1)
-        g.vector.memset(T.ZC[0:CB, CB:2 * CB], 0.0).then_inc(S.ms, 1)
     g.wait_ge(S.ld, 16)
-    for call in XS[r]:
-        fused([(d, ne, X[:, 0], X[:, slot_at(d, r)], S["a%d" % slot_at(d, r)]) for d, ne in call])
-
-    fams = sorted(["I", "R"], key=lambda f: ready(r, f))
-    F = {"R": dict(guests=R[r], s0=2, lo=CB, oc=0), "I": dict(guests=I[r], s0=4, lo=0, oc=2 * CB)}
+    fused([x_to(C[r]), x_to(OUT[r][0])])
+    for d in OUT[r][1:]:
+        fused([x_to(d)])
 
     te, ve = g.tensor, g.vector
 
-    def group(out, lo, l, r0, r1, sem=None):
+    def group(out, lhs, rhs, sem=None):
         for t in range(KT):
-            rhs = X[:, r0:r1, t, :] if r1 - r0 > 1 else X[:, r0, t, :]
-            mm = te.matmul(out[lo:lo + CB, 0:CB * (r1 - r0)], X[:, l, t, :], rhs, t == 0, t == KT - 1)
+            mm = te.matmul(out, lhs(t), rhs(t), t == 0, t == KT - 1)
         if sem is not None:
             mm.then_inc(sem, 1)
 
-    def rounded(msem, csem, out, in_):
-        ve.wait_ge(msem, 1)
-        ve.tensor_copy(out, in_).then_inc(csem, 1)
+    def tile(sl):
+        return lambda t: X[:, sl, t, :]
 
+    na1 = len(x_engines(C[r], r))
+    ve.wait_ge(S.ld, 16)
+    ve.tensor_copy(XV[:, :, 0:CB], X[:, 0]).then_inc(S.iV, 1)
+    ve.tensor_copy(XV[:, :, 2 * CB:3 * CB], X[:, 0]).then_inc(S.iV, 1)
+    if n % 2:
+        ve.memset(T.ZC[CB:2 * CB, CB * (n // 2):CB * (n // 2) + CB], 0.0).then_inc(S.ms, 1)
+    ve.wait_ge(S.a1, na1)
+    ve.tensor_copy(XV[:, :, CB:2 * CB], X[:, 1]).then_inc(S.iV, 1)
     te.wait_ge(S.ld, 16)
-    te.wait_ge(S.a1, x_engines(C[r]))
-    for q, fn in enumerate(fams):
-        f = F[fn]
-        k, s0, lo = len(f["guests"]), f["s0"], f["lo"]
-        for j, s in enumerate(f["guests"]):
-            te.wait_ge(S["a%d" % (s0 + j)], x_engines(s))
-        for j in range(k):
-            group(T["pB" + fn], CB * j, s0 + j, 0, 2, S["mB" + fn] if j == k - 1 else None)
-        rounded(S["mB" + fn], S["cB" + fn], T["ZB" + fn][0:CB * k, :], T["pB" + fn][0:CB * k, 0:2 * CB])
-        group(T["pC" + fn], lo, 1, s0, s0 + k, S["mC" + fn])
-        rounded(S["mC" + fn], S["cC" + fn], T.ZC[lo:lo + CB, 0:CB * k], T["pC" + fn][lo:lo + CB, 0:CB * k])
-        group(T["pO" + fn], 0, 0, s0, s0 + k, S["mO" + fn])
-        rounded(S["mO" + fn], S["cO" + fn], T.ZO[0:CB, f["oc"]:f["oc"] + CB * k], T["pO" + fn][0:CB, 0:CB * k])
+    te.wait_ge(S.a1, na1)
+    for q, s in enumerate(guests):
+        sl, pB, pV = slot_at(r, s), T["pB%d" % q], T["pV%d" % q]
+        te.wait_ge(S["a%d" % sl], len(x_engines(s, r)))
+        group(pB[0:CB, 0:CB], tile(sl), tile(0))
+        group(pB[CB:2 * CB, 0:CB], tile(sl), tile(1), S["mB%d" % q])
+        ve.wait_ge(S["mB%d" % q], 1)
+        ve.tensor_copy(T.ZB[:, q, :], pB[:, 0:CB]).then_inc(S["cB%d" % q], 1)
         if q == 0:
-            group(T.p1, 0, 0, 1, 2, S.m1)
-            rounded(S.m1, S.c1, T.ZO[0:CB, 4 * CB:5 * CB], T.p1[0:CB, 0:CB])
+            te.wait_ge(S.iV, 3)
+        hc, ho, cc = CB * (q % 2), CB * (1 - q % 2), CB * (q // 2)
+        group(pV[:, 0:CB], lambda t, lo=ho: XV[:, t, lo:lo + 2 * CB], tile(sl), S["mV%d" % q])
+        ve.wait_ge(S["mV%d" % q], 1)
+        ve.tensor_copy(T.ZC[hc:hc + CB, cc:cc + CB], pV[hc:hc + CB, 0:CB]).then_inc(S["cC%d" % q], 1)
+        ve.tensor_copy(T.ZO[ho:ho + CB, CB * q:CB * q + CB], pV[ho:ho + CB, 0:CB]).then_inc(S["cV%d" % q], 1)
+    te.wait_ge(S.cB0, 1)
+    group(T.pB0[0:CB, 0:CB], tile(0), tile(1), S.m1)
+    ve.wait_ge(S.m1, 1)
+    ve.tensor_copy(T.Z1[0:CB, :], T.pB0[0:CB, 0:CB]).then_inc(S.c1, 1)
 
-    for fn in fams:
-        g.wait_ge(S["cB" + fn], 1)
-        if fn == "R":
-            fused([(d, 4, T.ZBR[:, :], T.LR[:, W2[d].index(r)], S["rR%d" % W2[d].index(r)]) for d in R[r]])
-        else:
-            if ni == 1:
-                g.wait_ge(S.ms, 2)
-            fused([(d, 8 // ni, T.ZBI[:, :], T.LI[:, W3[d].index(r)], S["rI%d" % W3[d].index(r)]) for d in I[r]])
-    g.wait_ge(S.cCR, 1)
-    g.wait_ge(S.cCI, 1)
-    fused([(C[r], 8, T.ZC[:, :], T.LC[:, :], S.rC)])
+    for q, s in enumerate(guests):
+        j = HS[s].index(r)
+        g.wait_ge(S["cB%d" % q], 1)
+        fused([(s, engines(r, s), T.ZB[:, q, :], T.LB[:, j, :], S["rB%d" % j])])
+        if q == 1:
+            g.wait_ge(S.cC0, 1)
+            g.wait_ge(S.cC1, 1)
+            fused([(C[r], engines(r, C[r]), T.ZC[:, 0:CB], T.LC[:, 0:CB], S.rC0)])
+    for q in range(2, n):
+        g.wait_ge(S["cC%d" % q], 1)
+    if n % 2:
+        g.wait_ge(S.ms, 1)
+    fused([(C[r], engines(r, C[r]), T.ZC[:, CB:2 * CB], T.LC[:, CB:2 * CB], S.rC1)])
 
-    nst = [0]
-    qs = [g.sync, g.scalar]
-
-    def store(sem, val, pieces):
-        for s, src, k in pieces:
-            q = qs[nst[0] % 2]
-            q.wait_ge(sem, val)
-            q.dma_start(T.y[:, CB * s:CB * (s + k)], src).then_inc(S.st, 16)
-            nst[0] += 1
-
-    def runs(blocks, tile, lo, off):
-        out, j = [], 0
-        while j < len(blocks):
-            k = 1
-            while j + k < len(blocks) and blocks[j + k] == blocks[j] + k:
-                k += 1
-            out.append((blocks[j], tile[lo:lo + CB, off + CB * j:off + CB * (j + k)], k))
-            j += k
-        return out
-
-    for q, fn in enumerate(fams):
-        store(S["cO" + fn], 1, runs(F[fn]["guests"], T.ZO, 0, F[fn]["oc"]))
-        if q == 0:
-            store(S.c1, 1, runs([C[r]], T.ZO, 0, 4 * CB))
-    back = []
-    for j, v in enumerate(W2[r]):
-        lo = CB * R[v].index(r)
-        back.append(((ready(v, "R"), 0, v), S["rR%d" % j], 4,
-                     [(v, T.LR[lo:lo + CB, j, 0:CB], 1), (C[v], T.LR[lo:lo + CB, j, CB:2 * CB], 1)]))
-    for j, v in enumerate(W3[r]):
-        lo = CB * I[v].index(r)
-        back.append(((ready(v, "I"), 0, v), S["rI%d" % j], 8 // len(I[v]),
-                     [(v, T.LI[lo:lo + CB, j, 0:CB], 1), (C[v], T.LI[lo:lo + CB, j, CB:2 * CB], 1)]))
+    jobs = []
+    for q, s in enumerate(guests):
+        ho = CB * (1 - q % 2)
+        jobs.append((q + 1.0, [(S["cV%d" % q], 1)], s, T.ZO[ho:ho + CB, CB * q:CB * q + CB]))
+    jobs.append((n + 0.5, [(S.c1, 1)], C[r], T.Z1[0:CB, :]))
+    for j, v in enumerate(HS[r]):
+        w = [(S["rB%d" % j], len(engines(v, r)))]
+        when = ORD[v].index(r) + 2.5
+        jobs.append((when, w, v, T.LB[0:CB, j, :]))
+        jobs.append((when, w, C[v], T.LB[CB:2 * CB, j, :]))
     v = C[r]
-    back.append(((max(ready(v, "R"), ready(v, "I")), 1, v), S.rC, 8, runs(R[v], T.LC, CB, 0) + runs(I[v], T.LC, 0, 0)))
-    for key, sem, val, pieces in sorted(back, key=lambda b: b[0]):
-        store(sem, val, pieces)
+    nv, ne = len(ORD[v]), len(engines(v, r))
+    for q, s in enumerate(ORD[v]):
+        hc, cc = CB * (q % 2), CB * (q // 2)
+        jobs.append(((1 if q < 2 else nv - 1) + 3.0, [(S.rC0 if q < 2 else S.rC1, ne)], s, T.LC[hc:hc + CB, cc:cc + CB]))
+    queues = [g.sync, g.scalar]
+    for i, (when, waits, s, src) in enumerate(sorted(jobs, key=lambda b: (b[0], b[2]))):
+        q = queues[i % 2]
+        for sem, val in waits:
+            q.wait_ge(sem, val)
+        q.dma_start(T.y[:, CB * s:CB * (s + 1)], src).then_inc(S.st, 16)
 
     g.wait_ge(S.snt, sent[0])
-    g.wait_ge(S.st, 16 * nst[0])
+    g.wait_ge(S.st, 16 * len(jobs))

from concourse.bass import DstId, RemoteDMATransfer

KT, CB, NG = 8, 64, 4
SCRATCH = {
    "X": ("sbuf", [128, 6, KT, CB], "bfloat16"),
    "XV": ("sbuf", [128, KT, 3 * CB], "bfloat16"),
    "ZB": ("sbuf", [128, NG, CB], "bfloat16"),
    "ZO": ("sbuf", [128, NG * CB], "bfloat16"),
    "ZC": ("sbuf", [128, 2 * CB], "bfloat16"),
    "Z1": ("sbuf", [128, CB], "bfloat16"),
    "LB": ("sbuf", [128, NG, CB], "bfloat16"),
    "LC": ("sbuf", [128, 2 * CB], "bfloat16"),
}
SEMAPHORES = ["ld", "a1", "a2", "a3", "a4", "a5", "snt", "iV", "ms", "m1", "c1", "rC0", "rC1", "st"]
for _q in range(NG):
    SCRATCH["pB%d" % _q] = ("psum", [128, 512], "float32")
    SCRATCH["pV%d" % _q] = ("psum", [128, 512], "float32")
    SEMAPHORES += ["mB%d" % _q, "mV%d" % _q, "cB%d" % _q, "cV%d" % _q, "cC%d" % _q, "rB%d" % _q]
_CACHE = {}


def _bits(m):
    return [e for e in range(32) if (m >> e) & 1]


def _plan(cores, topo):
    if "p" in _CACHE:
        return _CACHE["p"]
    n = len(cores)
    rk = range(n)
    host = [topo.host(c) for c in cores]
    rack = [topo.rack(h) for h in host]
    same_host = lambda a, b: host[a] == host[b]
    C = [[s for s in rk if rack[s] != rack[r] and topo.may_write(cores[r], cores[s]) and topo.chip(cores[s]) == topo.chip(cores[r])][0]
         for r in rk]
    mine = [[s for s in rk if same_host(r, s)] for r in rk]
    half = [int(not any(topo.mates(cores[r], cores[s]) for s in mine[r])) for r in rk]
    pos = [mine[r].index(r) for r in rk]
    low = [host[r] in (host[0], host[C[0]]) for r in rk]
    nb = [[s for s in rk if rack[s] == rack[r] and not same_host(r, s)] for r in rk]
    W2 = [[s for s in nb[r] if (half[s] != half[r]) == low[r]] for r in rk]

    def route(a, b):
        ca, cb = cores[a], cores[b]
        if rack[a] != rack[b]:
            return [("cable", a)]
        if topo.mates(ca, cb):
            return [("mate", a)]
        if topo.same_plane(ca, cb):
            return [("out", a), ("in", b)]
        m = [s for s in mine[a] if topo.mates(ca, cores[s])]
        return [("mate", a), ("out", m[0] if m else ("mate of", a)), ("in", b)]

    k = len(mine[0])
    pairs = [(i, j) for i in range(k) for j in range(i + 1, k)]
    best = None
    for code in range(1 << len(pairs)):
        arcs = [(p if (code >> q) & 1 else (p[1], p[0])) for q, p in enumerate(pairs)]
        sends = [(r, C[r]) for r in rk] + [(r, s) for r in rk for s in W2[r]]
        sends += [(mine[r][i], mine[r][j]) for r in rk if pos[r] == 0 for i, j in arcs]
        load, got = {}, [0] * n
        for a, b in sends:
            got[b] += 1
            for l in route(a, b):
                load[l] = load.get(l, 0) + 1
        top = lambda kind: max(v for l, v in load.items() if l[0] == kind)
        score = (max(got), top("in"), top("out"), top("mate"), sum(v * v for v in load.values()), code)
        if best is None or score < best[0]:
            best = (score, arcs)
    arcs = best[1]
    W3 = [sorted(mine[r][j] for i, j in arcs if i == pos[r]) for r in rk]
    R = [[s for s in rk if r in W2[s]] for r in rk]
    I = [[s for s in rk if r in W3[s]] for r in rk]
    HS = [W2[r] + W3[r] for r in rk]
    GS = [R[r] + I[r] for r in rk]
    edges = [(s, d) for s in rk for d in HS[s]]
    turn = {}

    def colour(i):
        if i == len(edges):
            return True
        s, d = edges[i]
        for c in range(min(len(HS[s]), len(GS[d]))):
            if all(turn[e] != c for e in edges[:i] if e[0] == s or e[1] == d):
                turn[(s, d)] = c
                if colour(i + 1):
                    return True
                del turn[(s, d)]
        return False

    assert colour(0)
    OUT = [sorted(HS[r], key=lambda d: turn[(r, d)]) for r in rk]
    ORD = [sorted(GS[r], key=lambda s: turn[(s, r)]) for r in rk]
    p = {"C": C, "R": R, "I": I, "HS": HS, "OUT": OUT, "ORD": ORD}
    _CACHE["p"] = p
    return p


def rank_program(g, core, T, topo):
    r = T.rank_of(core)
    if r is None:
        return
    cores = list(T.cores)
    P = _plan(cores, topo)
    C, R, I, HS, OUT, ORD = P["C"], P["R"], P["I"], P["HS"], P["OUT"], P["ORD"]
    S = T.sem
    X, XV = T.X, T.XV
    guests = ORD[r]
    n = len(guests)
    sent = [0]

    def slot_at(v, s):
        return 1 if s == C[v] else (2 + R[v].index(s) if s in R[v] else 4 + I[v].index(s))

    def engines(a, b, j=0, m=1):
        return _bits(topo.mask(cores[a], cores[b]))[j::m]

    def x_engines(s, d):
        if d == C[s]:
            return engines(s, d, 0, 2)
        return engines(s, d, 1, 2) if d == OUT[s][0] else engines(s, d)

    def fused(items):
        trs = []
        for d, eng, src, dst, sem in items:
            rid, pid = topo.addr(cores[d], core)
            trs.append(RemoteDMATransfer(dst_ids=[DstId(rid=rid, pnc=pid)], dma_engine_mask=sum(1 << e for e in eng),
                                         remote_sem=sem, src=src, dst=dst))
            sent[0] += len(eng)
        g.remote_dma_fused(trs, local_sem=S.snt)

    def x_to(d):
        return (d, x_engines(r, d), X[:, 0], X[:, slot_at(d, r)], S["a%d" % slot_at(d, r)])

    g.sync.dma_start(X[:, 0], T.x[:]).then_inc(S.ld, 16)
    g.wait_ge(S.ld, 16)
    fused([x_to(C[r]), x_to(OUT[r][0])])
    for d in OUT[r][1:]:
        fused([x_to(d)])

    te, ve = g.tensor, g.vector

    def group(out, lhs, rhs, sem=None):
        for t in range(KT):
            mm = te.matmul(out, lhs(t), rhs(t), t == 0, t == KT - 1)
        if sem is not None:
            mm.then_inc(sem, 1)

    def tile(sl):
        return lambda t: X[:, sl, t, :]

    na1 = len(x_engines(C[r], r))
    ve.wait_ge(S.ld, 16)
    ve.tensor_copy(XV[:, :, 0:CB], X[:, 0]).then_inc(S.iV, 1)
    ve.tensor_copy(XV[:, :, 2 * CB:3 * CB], X[:, 0]).then_inc(S.iV, 1)
    if n % 2:
        ve.memset(T.ZC[CB:2 * CB, CB * (n // 2):CB * (n // 2) + CB], 0.0).then_inc(S.ms, 1)
    ve.wait_ge(S.a1, na1)
    ve.tensor_copy(XV[:, :, CB:2 * CB], X[:, 1]).then_inc(S.iV, 1)
    te.wait_ge(S.ld, 16)
    te.wait_ge(S.a1, na1)
    for q, s in enumerate(guests):
        sl, pB, pV = slot_at(r, s), T["pB%d" % q], T["pV%d" % q]
        te.wait_ge(S["a%d" % sl], len(x_engines(s, r)))
        group(pB[0:CB, 0:CB], tile(sl), tile(0))
        group(pB[CB:2 * CB, 0:CB], tile(sl), tile(1), S["mB%d" % q])
        ve.wait_ge(S["mB%d" % q], 1)
        ve.tensor_copy(T.ZB[:, q, :], pB[:, 0:CB]).then_inc(S["cB%d" % q], 1)
        if q == 0:
            te.wait_ge(S.iV, 3)
        hc, ho, cc = CB * (q % 2), CB * (1 - q % 2), CB * (q // 2)
        group(pV[:, 0:CB], lambda t, lo=ho: XV[:, t, lo:lo + 2 * CB], tile(sl), S["mV%d" % q])
        ve.wait_ge(S["mV%d" % q], 1)
        ve.tensor_copy(T.ZC[hc:hc + CB, cc:cc + CB], pV[hc:hc + CB, 0:CB]).then_inc(S["cC%d" % q], 1)
        ve.tensor_copy(T.ZO[ho:ho + CB, CB * q:CB * q + CB], pV[ho:ho + CB, 0:CB]).then_inc(S["cV%d" % q], 1)
    te.wait_ge(S.cB0, 1)
    group(T.pB0[0:CB, 0:CB], tile(0), tile(1), S.m1)
    ve.wait_ge(S.m1, 1)
    ve.tensor_copy(T.Z1[0:CB, :], T.pB0[0:CB, 0:CB]).then_inc(S.c1, 1)

    for q, s in enumerate(guests):
        j = HS[s].index(r)
        g.wait_ge(S["cB%d" % q], 1)
        fused([(s, engines(r, s), T.ZB[:, q, :], T.LB[:, j, :], S["rB%d" % j])])
        if q == 1:
            g.wait_ge(S.cC0, 1)
            g.wait_ge(S.cC1, 1)
            fused([(C[r], engines(r, C[r]), T.ZC[:, 0:CB], T.LC[:, 0:CB], S.rC0)])
    for q in range(2, n):
        g.wait_ge(S["cC%d" % q], 1)
    if n % 2:
        g.wait_ge(S.ms, 1)
    fused([(C[r], engines(r, C[r]), T.ZC[:, CB:2 * CB], T.LC[:, CB:2 * CB], S.rC1)])

    jobs = []
    for q, s in enumerate(guests):
        ho = CB * (1 - q % 2)
        jobs.append((q + 1.0, [(S["cV%d" % q], 1)], s, T.ZO[ho:ho + CB, CB * q:CB * q + CB]))
    jobs.append((n + 0.5, [(S.c1, 1)], C[r], T.Z1[0:CB, :]))
    for j, v in enumerate(HS[r]):
        w = [(S["rB%d" % j], len(engines(v, r)))]
        when = ORD[v].index(r) + 2.5
        jobs.append((when, w, v, T.LB[0:CB, j, :]))
        jobs.append((when, w, C[v], T.LB[CB:2 * CB, j, :]))
    v = C[r]
    nv, ne = len(ORD[v]), len(engines(v, r))
    for q, s in enumerate(ORD[v]):
        hc, cc = CB * (q % 2), CB * (q // 2)
        jobs.append(((1 if q < 2 else nv - 1) + 3.0, [(S.rC0 if q < 2 else S.rC1, ne)], s, T.LC[hc:hc + CB, cc:cc + CB]))
    queues = [g.sync, g.scalar]
    for i, (when, waits, s, src) in enumerate(sorted(jobs, key=lambda b: (b[0], b[2]))):
        q = queues[i % 2]
        for sem, val in waits:
            q.wait_ge(sem, val)
        q.dma_start(T.y[:, CB * s:CB * (s + 1)], src).then_inc(S.st, 16)

    g.wait_ge(S.snt, sent[0])
    g.wait_ge(S.st, 16 * len(jobs))
